import numpy as np
import ml_dtypes


def mxq(x, axis, fmt="e4m3"):
    dtype, down = {"e4m3": (ml_dtypes.float8_e4m3fn, 7), "e5m2": (ml_dtypes.float8_e5m2, 14)}[fmt]
    v = np.moveaxis(np.asarray(x, np.float32).astype(ml_dtypes.bfloat16).astype(np.float64), axis, -1)
    blocks = v.reshape(v.shape[:-1] + (-1, 32))
    amax = np.abs(blocks).max(-1, keepdims=True)
    byte = np.maximum(np.where(amax > 0, np.frexp(amax)[1] - 1 + 127, 0) - down, 1)
    scale = np.exp2(byte - 127.0)
    codes = (blocks / scale).astype(np.float32).astype(dtype).astype(np.float64)
    return np.moveaxis((codes * scale).reshape(v.shape), -1, axis)


WIDE = False


def mx_kscale(k):
    if not WIDE:
        return np.ones(k)
    levels = np.array([10, -10, 5, -5, 0])
    if k % 512:
        return np.exp2(np.random.permutation(np.resize(levels, k // 32))).repeat(32)
    a = np.empty((k // 512, 16))
    for p in range(k // 512):
        a[p, :8] = np.random.permutation(np.resize(levels, 8))
        for g in range(8):
            far = levels[np.abs(levels - a[p, g]) >= 10]
            a[p, g + 8] = far[np.random.randint(len(far))]
    return np.exp2(a.ravel()).repeat(32)


def f64(x):
    return np.asarray(x).astype(np.float64)


def striped(idx):
    return np.tile(idx.reshape(-1, 16).T, (8, 1)).astype(np.uint16)


def unstriped(offs):
    return offs[:16].T.reshape(-1).astype(np.int64)


E2M1 = np.array([0.0, 0.5, 1.0, 1.5, 2.0, 3.0, 4.0, 6.0, -0.0, -0.5, -1.0, -1.5, -2.0, -3.0, -4.0, -6.0])


def pack_weight(w, fmt):
    k, n = w.shape
    w = f64(np.asarray(w, np.float32).astype(ml_dtypes.bfloat16)).reshape(k // 32, 32, n)
    amax = np.abs(w).max(1)
    if fmt == "e4m3":
        byte = np.frexp(amax)[1] - 1 + 127 - 7
    else:
        mant, ex = np.frexp(amax / 6.0)
        byte = np.where(mant > 0.5, ex, ex - 1) + 127
    byte = np.clip(np.where(amax > 0, byte, 1), 1, 254)
    scaled = (w * np.exp2(127.0 - byte)[:, None, :]).reshape(k, n).astype(np.float32)
    by_word = np.ascontiguousarray(scaled.reshape(k // 512, 128, 4, n).transpose(0, 1, 3, 2))
    if fmt == "e4m3":
        words = by_word.astype(ml_dtypes.float8_e4m3fn).view(np.uint8)
    else:
        c = by_word.astype(ml_dtypes.float4_e2m1fn).view(np.uint8) & 0xF
        words = (c[..., 0::2] | (c[..., 1::2] << 4)).reshape(k // 512, 128, 2 * n)
    return np.ascontiguousarray(words), np.ascontiguousarray(byte.astype(np.uint8).reshape(k // 512, 16, n))


def unpack_weight(words, scales, fmt):
    g, _, n = scales.shape
    words = np.ascontiguousarray(words).reshape(g, 128, n, -1)
    if fmt == "e4m3":
        vals = words.view(ml_dtypes.float8_e4m3fn).astype(np.float64)
    else:
        nib = np.empty((g, 128, n, 4), np.uint8)
        nib[..., 0::2] = words & 0xF
        nib[..., 1::2] = words >> 4
        vals = E2M1[nib]
    vals = vals * np.repeat(np.exp2(scales.astype(np.float64) - 127.0), 8, axis=1)[..., None]
    return vals.transpose(0, 1, 3, 2).reshape(g * 512, n)


def relu(v):
    return np.maximum(v, 0.0)


K, T, E, C, N = 1536, 1280, 10, 256, 128


def by_expert(wq, xq):
    return np.concatenate([wq[e].T @ xq[:, e * C:(e + 1) * C] for e in range(E)], axis=1)


def setup_inputs():
    n = np.random.standard_normal
    s = mx_kscale(K)[:, None]
    first = np.random.permutation(np.repeat(np.arange(E), T // E))
    second = (first + 1 + np.random.permutation(np.repeat(np.arange(E - 1), -(-T // (E - 1)))[:T])) % E
    while np.bincount(second, minlength=E).max() != T // E:
        load = np.bincount(second, minlength=E); hi, lo = int(load.argmax()), int(load.argmin())
        t = np.flatnonzero((second == hi) & (first != lo))[0]; second[t] = lo
    slot_token = np.empty(E * C, np.int64); pos = np.empty((2, T), np.int64); fill = np.zeros(E, np.int64)
    place = np.stack([np.random.permutation(C) for _ in range(E)])
    for r, deal in enumerate((first, second)):
        for t in np.random.permutation(T):
            e = deal[t]; j = e * C + place[e, fill[e]]; fill[e] += 1; slot_token[j] = t; pos[r, t] = j
    g = np.random.uniform(0.2, 0.8, T)
    x = pack_weight(n((K, T)) * s, "e4m3")
    return {
        "x_words": x[0],
        "x_scales": x[1],
        "w": (n((E + 1, K, N)) / np.sqrt(K) / s[None]).astype(np.float32),
        "b": (0.3 * n((N, E + 1))).astype(np.float32),
        "gate": np.stack([np.tile(g, (N, 1)), np.tile(1.0 - g, (N, 1))]).astype(np.float32),
        "offs": striped(slot_token),
        "pos1": striped(pos[0]),
        "pos2": striped(pos[1]),
    }


def reference(x_words, x_scales, w, b, gate, offs, pos1, pos2):
    idx = unstriped(offs)
    wq = mxq(f64(w), 1, "e4m3")
    xs = unpack_weight(x_words, x_scales, "e4m3")
    ys = relu((wq[E].T @ xs) + f64(b)[:, E:])
    xq = unpack_weight(x_words, x_scales, "e4m3")[:, idx]
    y = by_expert(wq, xq)
    y = relu(y + np.repeat(f64(b)[:, :E], C, axis=1))
    return ys + f64(gate[0]) * y[:, unstriped(pos1)] + f64(gate[1]) * y[:, unstriped(pos2)]

@@ -1,0 +1,173 @@
+from contextlib import ExitStack
+
+import concourse.mybir as mybir
+from concourse.masks import make_identity
+
+K, T, E, C, N = 1536, 1280, 10, 256, 128
+S = E * C
+FLOPS = 2 * K * N * (S + T)
+
+F32 = mybir.dt.float32
+BF16 = mybir.dt.bfloat16
+I32 = mybir.dt.int32
+U32 = mybir.dt.uint32
+U16 = mybir.dt.uint16
+U8 = mybir.dt.uint8
+FP8X4 = mybir.dt.float8_e4m3fn_x4
+RELU = mybir.ActivationFunctionType.Relu
+MULT = mybir.AluOpType.mult
+ADD = mybir.AluOpType.add
+
+P = 128
+PACK = 4
+PASSES = K // (P * PACK)
+LANES = 16
+GATHER_CUTS = (0, 960, 1920, 2560)
+LAST_CUTS = (0, 960, 1920, 2304, 2560)
+TOKEN_CUTS = (0, 512, 1024, 1280)
+SUM_CUTS = (0, 512, 896, 1024)
+
+
+def tile_moe_shr_lin_relu_kernel(tc, x_words, x_scales, w, b, gate, offs, pos1, pos2, out):
+    nc = tc.nc
+    with ExitStack() as ctx:
+        keep = ctx.enter_context(tc.tile_pool(name="keep", bufs=1))
+        psum = ctx.enter_context(tc.psum_pool(name="psum", bufs=1))
+
+        offs_sb = keep.tile([P, S // LANES], U16, name="offs_sb")
+        pos1_sb = keep.tile([P, T // LANES], U16, name="pos1_sb")
+        pos2_sb = keep.tile([P, T // LANES], U16, name="pos2_sb")
+        x_sb = [keep.tile([P, T], I32, name="x_sb%d" % o, align_bytes=64) for o in range(PASSES)]
+        xs_sb = keep.tile([P, T], U8, name="xs_sb", align_bytes=64)
+        raw = [keep.tile([P, PASSES, PACK, N], F32, name="raw%d" % e, tag="raw%d" % e, align_bytes=64) for e in range(E + 1)]
+        b_sb = keep.tile([P, E + 1], F32, name="b_sb")
+        gate_sb = [keep.tile([P, T], F32, name="gate_sb%d" % r) for r in range(2)]
+
+        def load_x(o):
+            nc.sync.dma_start(x_sb[o][:], x_words[o].rearrange("p t r -> p (t r)").bitcast(I32))
+
+        def load_w(e):
+            nc.sync.dma_start(raw[e][:], w[e].rearrange("(o p j) n -> p o j n", o=PASSES, j=PACK))
+
+        ident = keep.tile([P, P], F32, name="ident")
+        make_identity(nc, ident[:])
+        nc.vector.memset(xs_sb[:].bitcast(I32), 0)
+        nc.sync.dma_start(offs_sb[:], offs)
+        load_x(0)
+        for q in range(4):
+            nc.scalar.dma_start(
+                xs_sb[32 * q : 32 * q + 4 * PASSES, :].bitcast(I32),
+                x_scales[:, 4 * q : 4 * q + 4, :].bitcast(I32),
+            )
+        for e in range(0, 4):
+            load_w(e)
+        load_x(1)
+        for e in range(4, 7):
+            load_w(e)
+        load_x(2)
+        for e in range(7, E):
+            load_w(e)
+        nc.sync.dma_start(b_sb[:], b)
+        load_w(E)
+        nc.sync.dma_start(pos1_sb[:], pos1)
+        nc.sync.dma_start(pos2_sb[:], pos2)
+        for r in range(2):
+            nc.sync.dma_start(gate_sb[r][:], gate[r])
+
+        g_words = [keep.tile([P, S], U32, name="g_words%d" % o, align_bytes=64) for o in range(PASSES)]
+        g_scales = keep.tile([P, S], U8, name="g_scales", align_bytes=64)
+
+        def gather(dst, window, cuts):
+            for lo, hi in zip(cuts[:-1], cuts[1:]):
+                nc.vector.tensor_copy(dst[:, lo:hi], window.indirect(offs_sb[:, lo // LANES : hi // LANES]))
+
+        w_codes = [keep.tile([P, PASSES * N], U32, name="w_codes%d" % e, align_bytes=64) for e in range(E + 1)]
+        w_scales = [keep.tile([P, PASSES * N], U8, name="w_scales%d" % e, align_bytes=64) for e in range(E + 1)]
+        grouped = [keep.tile([P, K], BF16, name="grouped%d" % e, align_bytes=64) for e in range(E + 1)]
+
+        def cast(e):
+            nc.scalar.copy(
+                grouped[e][:].rearrange("p (o c i j) -> p o c j i", o=PASSES, i=4, j=PACK),
+                raw[e][:].rearrange("p o j (c i) -> p o c j i", i=4),
+            )
+
+        def quantize(e):
+            for lo, hi in ((0, 1024), (1024, K)):
+                nc.vector.quantize_mx(
+                    out=w_codes[e][:, lo // PACK : hi // PACK].bitcast(FP8X4),
+                    scales=w_scales[e][:, lo // PACK : hi // PACK],
+                    in_=grouped[e][:, lo:hi],
+                )
+
+        def multiply(acc, e, words, scales, cols):
+            for o in range(PASSES):
+                nc.tensor.matmul_mx(
+                    out=acc,
+                    lhsT=w_codes[e][:, o * N : (o + 1) * N].bitcast(FP8X4),
+                    lhsT_scale=w_scales[e][:, o * N : (o + 1) * N],
+                    rhs=words[o][:, cols].bitcast(FP8X4),
+                    rhs_scale=scales[4 * o : P, cols],
+                    start=(o == 0),
+                    stop=(o == PASSES - 1),
+                )
+
+        for e in range(E + 1):
+            cast(e)
+        gather(g_words[0], x_sb[0][:].bitcast(U32), GATHER_CUTS)
+        gather(g_scales, xs_sb[:], GATHER_CUTS)
+        for e in range(0, 4):
+            quantize(e)
+        gather(g_words[1], x_sb[1][:].bitcast(U32), GATHER_CUTS)
+        for e in range(4, E):
+            quantize(e)
+        gather(g_words[2], x_sb[2][:].bitcast(U32), LAST_CUTS)
+        quantize(E)
+
+        y = keep.tile([P, S], F32, name="y", tag="raw%d" % (E - 1), align_bytes=64)
+        for e in range(E):
+            acc = psum.tile([P, C], F32, name="acc", tag="acc", bufs=5)
+            cols = slice(e * C, (e + 1) * C)
+            multiply(acc[:], e, g_words, g_scales, cols)
+            nc.scalar.activation(y[:, cols], acc[:], RELU, bias=b_sb[:, e : e + 1])
+
+        ys = keep.tile([P, T], F32, name="ys")
+        token_cols = [slice(lo, hi) for lo, hi in zip(TOKEN_CUTS[:-1], TOKEN_CUTS[1:])]
+        for cols in token_cols:
+            acc_s = psum.tile([P, 512], F32, name="acc_s", tag="acc_s", bufs=3)
+            width = cols.stop - cols.start
+            multiply(acc_s[:, :width], E, x_sb, xs_sb, cols)
+            nc.scalar.activation(ys[:, cols], acc_s[:, :width], RELU, bias=b_sb[:, E : E + 1])
+
+        t1 = keep.tile([P, T], F32, name="t1")
+        t2 = keep.tile([P, T], F32, name="t2")
+        turned = keep.tile([P, T], F32, name="turned")
+        res = keep.tile([P, T], F32, name="res")
+
+        def products(cols):
+            lists = slice(cols.start // LANES, cols.stop // LANES)
+            nc.vector.tensor_tensor(t1[:, cols], y[:].indirect(pos1_sb[:, lists]), gate_sb[0][:, cols], MULT)
+            nc.vector.tensor_tensor(t2[:, cols], y[:].indirect(pos2_sb[:, lists]), gate_sb[1][:, cols], MULT)
+
+        for lo, hi in zip(SUM_CUTS[:-1], SUM_CUTS[1:]):
+            cols = slice(lo, hi)
+            width = hi - lo
+            products(cols)
+            total = psum.tile([P, 512], F32, name="total", tag="acc", bufs=5)
+            steps = [(term, c) for term in (ys, t1, t2) for c in range(0, width, P)]
+            for i, (term, c) in enumerate(steps):
+                nc.tensor.matmul(
+                    total[:, c : c + P], term[:, lo + c : lo + c + P], ident[:],
+                    is_transpose=True, start=(i == 0), stop=(i == len(steps) - 1),
+                )
+            nc.scalar.copy(turned[:, cols], total[:, :width])
+            back = psum.tile([P, 512], F32, name="back", tag="acc", bufs=5)
+            for c in range(0, width, P):
+                nc.tensor.transpose(back[:, c : c + P], turned[:, lo + c : lo + c + P], ident[:])
+            nc.scalar.copy(res[:, cols], back[:, :width])
+            nc.scalar.dma_start(out[:, cols], res[:, cols])
+
+        cols = slice(SUM_CUTS[-1], T)
+        products(cols)
+        nc.vector.tensor_tensor(turned[:, cols], t1[:, cols], ys[:, cols], ADD)
+        nc.vector.tensor_tensor(res[:, cols], turned[:, cols], t2[:, cols], ADD)
+        nc.sync.dma_start(out[:, cols], res[:, cols])

@@ -15,17 +15,26 @@ U16 = mybir.dt.uint16
 U8 = mybir.dt.uint8
 FP8X4 = mybir.dt.float8_e4m3fn_x4
 RELU = mybir.ActivationFunctionType.Relu
+COPY = mybir.ActivationFunctionType.Copy
 MULT = mybir.AluOpType.mult
 ADD = mybir.AluOpType.add
+MAX = mybir.AluOpType.max
 
 P = 128
 PACK = 4
 PASSES = K // (P * PACK)
 LANES = 16
+BANK = 512
 GATHER_CUTS = (0, 960, 1920, 2560)
-LAST_CUTS = (0, 960, 1920, 2304, 2560)
-TOKEN_CUTS = (0, 512, 1024, 1280)
-SUM_CUTS = (0, 512, 896, 1024)
+LAST_CUTS = (0, 960, 1920, 2304)
+TURNED = 896
+BLOCKS = TURNED // P
+FETCH_CUTS = (0, 512, 896)
+SUM_CUTS = (0, 512, 896)
+
+
+def pairs(cuts):
+    return list(zip(cuts[:-1], cuts[1:]))
 
 
 def tile_moe_shr_lin_relu_kernel(tc, x_words, x_scales, w, b, gate, offs, pos1, pos2, out):
@@ -34,14 +43,18 @@ def tile_moe_shr_lin_relu_kernel(tc, x_words, x_scales, w, b, gate, offs, pos1, 
         keep = ctx.enter_context(tc.tile_pool(name="keep", bufs=1))
         psum = ctx.enter_context(tc.psum_pool(name="psum", bufs=1))
 
+        def ring_bank(name):
+            return psum.tile([P, BANK], F32, name=name, tag="ring", bufs=8 - len(pairs(SUM_CUTS)))
+
         offs_sb = keep.tile([P, S // LANES], U16, name="offs_sb")
-        pos1_sb = keep.tile([P, T // LANES], U16, name="pos1_sb")
-        pos2_sb = keep.tile([P, T // LANES], U16, name="pos2_sb")
+        pos_sb = [keep.tile([P, T // LANES], U16, name="pos%d_sb" % r) for r in (1, 2)]
         x_sb = [keep.tile([P, T], I32, name="x_sb%d" % o, align_bytes=64) for o in range(PASSES)]
         xs_sb = keep.tile([P, T], U8, name="xs_sb", align_bytes=64)
         raw = [keep.tile([P, PASSES, PACK, N], F32, name="raw%d" % e, tag="raw%d" % e, align_bytes=64) for e in range(E + 1)]
         b_sb = keep.tile([P, E + 1], F32, name="b_sb")
-        gate_sb = [keep.tile([P, T], F32, name="gate_sb%d" % r) for r in range(2)]
+        gate_rows = keep.tile([P, P], F32, name="gate_rows")
+        gate_tail = keep.tile([P, 2, T - TURNED], F32, name="gate_tail")
+        ident = keep.tile([P, P], F32, name="ident")
 
         def load_x(o):
             nc.sync.dma_start(x_sb[o][:], x_words[o].rearrange("p t r -> p (t r)").bitcast(I32))
@@ -49,9 +62,9 @@ def tile_moe_shr_lin_relu_kernel(tc, x_words, x_scales, w, b, gate, offs, pos1, 
         def load_w(e):
             nc.sync.dma_start(raw[e][:], w[e].rearrange("(o p j) n -> p o j n", o=PASSES, j=PACK))
 
-        ident = keep.tile([P, P], F32, name="ident")
-        make_identity(nc, ident[:])
         nc.vector.memset(xs_sb[:].bitcast(I32), 0)
+        nc.gpsimd.memset(gate_rows[:], 0.0)
+        make_identity(nc, ident[:])
         nc.sync.dma_start(offs_sb[:], offs)
         load_x(0)
         for q in range(4):
@@ -59,31 +72,32 @@ def tile_moe_shr_lin_relu_kernel(tc, x_words, x_scales, w, b, gate, offs, pos1, 
                 xs_sb[32 * q : 32 * q + 4 * PASSES, :].bitcast(I32),
                 x_scales[:, 4 * q : 4 * q + 4, :].bitcast(I32),
             )
-        for e in range(0, 4):
-            load_w(e)
-        load_x(1)
-        for e in range(4, 7):
-            load_w(e)
-        load_x(2)
-        for e in range(7, E):
+        for e in (E, 0, 1):
             load_w(e)
         nc.sync.dma_start(b_sb[:], b)
-        load_w(E)
-        nc.sync.dma_start(pos1_sb[:], pos1)
-        nc.sync.dma_start(pos2_sb[:], pos2)
-        for r in range(2):
-            nc.sync.dma_start(gate_sb[r][:], gate[r])
+        nc.sync.dma_start(gate_rows[0 : 2 * BLOCKS, :], gate[:, 0, 0:TURNED].rearrange("r (c p) -> r c p", p=P))
+        load_w(2)
+        load_x(1)
+        for e in range(3, 6):
+            load_w(e)
+        load_x(2)
+        for e in range(6, E):
+            load_w(e)
+        nc.sync.dma_start(pos_sb[0][:], pos1)
+        nc.sync.dma_start(pos_sb[1][:], pos2)
+        nc.sync.dma_start(gate_tail[:], gate[:, :, TURNED:T].rearrange("r p t -> p r t"))
 
-        g_words = [keep.tile([P, S], U32, name="g_words%d" % o, align_bytes=64) for o in range(PASSES)]
+        g_words = [keep.tile([P, S], U32, name="g_words%d" % o, align_bytes=64) for o in range(PASSES - 1)]
+        g_words.append(keep.tile([P, S - C], U32, name="g_words_last", align_bytes=64))
         g_scales = keep.tile([P, S], U8, name="g_scales", align_bytes=64)
 
-        def gather(dst, window, cuts):
-            for lo, hi in zip(cuts[:-1], cuts[1:]):
-                nc.vector.tensor_copy(dst[:, lo:hi], window.indirect(offs_sb[:, lo // LANES : hi // LANES]))
+        def gather(dst, window, cuts, first=0):
+            for lo, hi in pairs(cuts):
+                nc.vector.tensor_copy(dst[:, lo - first : hi - first], window.indirect(offs_sb[:, lo // LANES : hi // LANES]))
 
         w_codes = [keep.tile([P, PASSES * N], U32, name="w_codes%d" % e, align_bytes=64) for e in range(E + 1)]
         w_scales = [keep.tile([P, PASSES * N], U8, name="w_scales%d" % e, align_bytes=64) for e in range(E + 1)]
-        grouped = [keep.tile([P, K], BF16, name="grouped%d" % e, align_bytes=64) for e in range(E + 1)]
+        grouped = [keep.tile([P, K], BF16, name="grouped%d" % e, tag="grouped%d" % e, align_bytes=64) for e in range(E + 1)]
 
         def cast(e):
             nc.scalar.copy(
@@ -105,69 +119,115 @@ def tile_moe_shr_lin_relu_kernel(tc, x_words, x_scales, w, b, gate, offs, pos1, 
                     out=acc,
                     lhsT=w_codes[e][:, o * N : (o + 1) * N].bitcast(FP8X4),
                     lhsT_scale=w_scales[e][:, o * N : (o + 1) * N],
-                    rhs=words[o][:, cols].bitcast(FP8X4),
+                    rhs=words[o].bitcast(FP8X4),
                     rhs_scale=scales[4 * o : P, cols],
                     start=(o == 0),
                     stop=(o == PASSES - 1),
                 )
 
-        for e in range(E + 1):
+        for e in [E] + list(range(E)):
             cast(e)
         gather(g_words[0], x_sb[0][:].bitcast(U32), GATHER_CUTS)
         gather(g_scales, xs_sb[:], GATHER_CUTS)
-        for e in range(0, 4):
+        for e in (E, 0, 1, 2):
             quantize(e)
         gather(g_words[1], x_sb[1][:].bitcast(U32), GATHER_CUTS)
-        for e in range(4, E):
+        for e in range(3, 6):
             quantize(e)
         gather(g_words[2], x_sb[2][:].bitcast(U32), LAST_CUTS)
-        quantize(E)
+        for e in range(6, E):
+            quantize(e)
+        g_end = keep.tile([P, C], U32, name="g_end", tag="grouped%d" % (E - 1), align_bytes=64)
+        gather(g_end, x_sb[2][:].bitcast(U32), (S - C, S), first=S - C)
 
-        y = keep.tile([P, S], F32, name="y", tag="raw%d" % (E - 1), align_bytes=64)
-        for e in range(E):
-            acc = psum.tile([P, C], F32, name="acc", tag="acc", bufs=5)
-            cols = slice(e * C, (e + 1) * C)
-            multiply(acc[:], e, g_words, g_scales, cols)
-            nc.scalar.activation(y[:, cols], acc[:], RELU, bias=b_sb[:, e : e + 1])
+        gate_bank = ring_bank("gate_bank")
+        nc.tensor.transpose(gate_bank[:, :P], gate_rows[:], ident[:])
+        gate_cols = keep.tile([P, 16], F32, name="gate_cols")
+        nc.scalar.copy(gate_cols[:], gate_bank[:, :16])
 
         ys = keep.tile([P, T], F32, name="ys")
-        token_cols = [slice(lo, hi) for lo, hi in zip(TOKEN_CUTS[:-1], TOKEN_CUTS[1:])]
-        for cols in token_cols:
-            acc_s = psum.tile([P, 512], F32, name="acc_s", tag="acc_s", bufs=3)
-            width = cols.stop - cols.start
-            multiply(acc_s[:, :width], E, x_sb, xs_sb, cols)
+        for lo in range(0, T, BANK):
+            cols = slice(lo, min(lo + BANK, T))
+            width = cols.stop - lo
+            acc_s = ring_bank("acc_s")
+            multiply(acc_s[:, :width], E, [x_sb[o][:, cols] for o in range(PASSES)], xs_sb, cols)
             nc.scalar.activation(ys[:, cols], acc_s[:, :width], RELU, bias=b_sb[:, E : E + 1])
-
-        t1 = keep.tile([P, T], F32, name="t1")
-        t2 = keep.tile([P, T], F32, name="t2")
-        turned = keep.tile([P, T], F32, name="turned")
-        res = keep.tile([P, T], F32, name="res")
-
-        def products(cols):
-            lists = slice(cols.start // LANES, cols.stop // LANES)
-            nc.vector.tensor_tensor(t1[:, cols], y[:].indirect(pos1_sb[:, lists]), gate_sb[0][:, cols], MULT)
-            nc.vector.tensor_tensor(t2[:, cols], y[:].indirect(pos2_sb[:, lists]), gate_sb[1][:, cols], MULT)
-
-        for lo, hi in zip(SUM_CUTS[:-1], SUM_CUTS[1:]):
-            cols = slice(lo, hi)
-            width = hi - lo
-            products(cols)
-            total = psum.tile([P, 512], F32, name="total", tag="acc", bufs=5)
-            steps = [(term, c) for term in (ys, t1, t2) for c in range(0, width, P)]
-            for i, (term, c) in enumerate(steps):
-                nc.tensor.matmul(
-                    total[:, c : c + P], term[:, lo + c : lo + c + P], ident[:],
-                    is_transpose=True, start=(i == 0), stop=(i == len(steps) - 1),
-                )
-            nc.scalar.copy(turned[:, cols], total[:, :width])
-            back = psum.tile([P, 512], F32, name="back", tag="acc", bufs=5)
+        ys_t = keep.tile([P, TURNED], F32, name="ys_t")
+        for lo in range(0, TURNED, BANK):
+            width = min(BANK, TURNED - lo)
+            ys_bank = ring_bank("ys_bank")
             for c in range(0, width, P):
-                nc.tensor.transpose(back[:, c : c + P], turned[:, lo + c : lo + c + P], ident[:])
-            nc.scalar.copy(res[:, cols], back[:, :width])
-            nc.scalar.dma_start(out[:, cols], res[:, cols])
+                nc.tensor.transpose(ys_bank[:, c : c + P], ys[:, lo + c : lo + c + P], ident[:])
+            nc.scalar.copy(ys_t[:, lo : lo + width], ys_bank[:, :width])
+        totals = {}
+        for lo, hi in pairs(SUM_CUTS):
+            totals[lo] = psum.tile([P, BANK], F32, name="total%d" % lo)
+            for c in range(lo, hi, P):
+                nc.tensor.matmul(
+                    totals[lo][:, c - lo : c - lo + P], ys_t[:, c : c + P], ident[:],
+                    is_transpose=True, start=(c == lo), stop=False,
+                )
 
-        cols = slice(SUM_CUTS[-1], T)
-        products(cols)
-        nc.vector.tensor_tensor(turned[:, cols], t1[:, cols], ys[:, cols], ADD)
-        nc.vector.tensor_tensor(res[:, cols], turned[:, cols], t2[:, cols], ADD)
-        nc.sync.dma_start(out[:, cols], res[:, cols])
+        y = keep.tile([P, S], F32, name="y", tag="raw%d" % (E - 1), align_bytes=64)
+        for e in range(E - 1):
+            acc = ring_bank("acc")
+            cols = slice(e * C, (e + 1) * C)
+            multiply(acc[:, :C], e, [g_words[o][:, cols] for o in range(PASSES)], g_scales, cols)
+            nc.scalar.activation(y[:, cols], acc[:, :C], RELU, bias=b_sb[:, e : e + 1])
+        for h in range(2):
+            acc = ring_bank("acc")
+            cols = slice(S - C + h * P, S - C + (h + 1) * P)
+            words = [g_words[0][:, cols], g_words[1][:, cols], g_end[:, h * P : (h + 1) * P]]
+            multiply(acc[:, :P], E - 1, words, g_scales, cols)
+            if h == 0:
+                nc.scalar.activation(y[:, cols], acc[:, :P], RELU, bias=b_sb[:, E - 1 : E])
+            else:
+                nc.vector.tensor_scalar(y[:, cols], acc[:, :P], b_sb[:, E - 1 : E], 0.0, ADD, MAX)
+
+        fetched = [keep.tile([P, T], F32, name="fetched%d" % r) for r in range(2)]
+        scaled = [keep.tile([P, TURNED], F32, name="scaled%d" % r) for r in range(2)]
+        res = keep.tile([P, T], F32, name="res")
+        for f_lo, f_hi in pairs(FETCH_CUTS):
+            for r in range(2):
+                nc.vector.tensor_copy(
+                    fetched[r][:, f_lo:f_hi], y[:].indirect(pos_sb[r][:, f_lo // LANES : f_hi // LANES])
+                )
+            chunks = [(lo, hi) for lo, hi in pairs(SUM_CUTS) if f_lo <= lo and hi <= f_hi]
+            for r in range(2):
+                for lo, hi in chunks:
+                    width = P if (r == 1 and hi == TURNED) else hi - lo
+                    for start in range(lo, hi, width):
+                        turned = ring_bank("turned")
+                        for c in range(start, start + width, P):
+                            nc.tensor.transpose(turned[:, c - start : c - start + P], fetched[r][:, c : c + P], ident[:])
+                        for c in range(start, start + width, P):
+                            col = BLOCKS * r + c // P
+                            nc.scalar.activation(
+                                scaled[r][:, c : c + P], turned[:, c - start : c - start + P], COPY,
+                                scale=gate_cols[:, col : col + 1],
+                            )
+                    for c in range(lo, hi, P):
+                        nc.tensor.matmul(
+                            totals[lo][:, c - lo : c - lo + P], scaled[r][:, c : c + P], ident[:],
+                            is_transpose=True, start=False, stop=(r == 1 and c == hi - P),
+                        )
+                    if r == 1:
+                        nc.scalar.copy(res[:, lo:hi], totals[lo][:, : hi - lo])
+                        queue = nc.scalar if hi == TURNED else nc.sync
+                        queue.dma_start(out[:, lo:hi], res[:, lo:hi])
+
+        def fetch_gated(r, lo, hi):
+            nc.vector.tensor_tensor(
+                fetched[r][:, lo:hi], y[:].indirect(pos_sb[r][:, lo // LANES : hi // LANES]),
+                gate_tail[:, r, lo - TURNED : hi - TURNED], MULT,
+            )
+
+        part = keep.tile([P, T - TURNED], F32, name="part")
+        mid = T - P
+        fetch_gated(0, TURNED, T)
+        fetch_gated(1, TURNED, mid)
+        nc.vector.tensor_tensor(part[:], fetched[0][:, TURNED:T], ys[:, TURNED:T], ADD)
+        fetch_gated(1, mid, T)
+        for lo, hi in ((TURNED, mid), (mid, T)):
+            nc.vector.tensor_tensor(res[:, lo:hi], part[:, lo - TURNED : hi - TURNED], fetched[1][:, lo:hi], ADD)
+            nc.sync.dma_start(out[:, lo:hi], res[:, lo:hi])

from contextlib import ExitStack

import concourse.mybir as mybir
from concourse.masks import make_identity

K, T, E, C, N = 1536, 1280, 10, 256, 128
S = E * C
FLOPS = 2 * K * N * (S + T)

F32 = mybir.dt.float32
BF16 = mybir.dt.bfloat16
I32 = mybir.dt.int32
U32 = mybir.dt.uint32
U16 = mybir.dt.uint16
U8 = mybir.dt.uint8
FP8X4 = mybir.dt.float8_e4m3fn_x4
RELU = mybir.ActivationFunctionType.Relu
COPY = mybir.ActivationFunctionType.Copy
MULT = mybir.AluOpType.mult
ADD = mybir.AluOpType.add
MAX = mybir.AluOpType.max

P = 128
PACK = 4
PASSES = K // (P * PACK)
LANES = 16
BANK = 512
GATHER_CUTS = (0, 960, 1920, 2560)
LAST_CUTS = (0, 960, 1920, 2304)
TURNED = 896
BLOCKS = TURNED // P
FETCH_CUTS = (0, 512, 896)
SUM_CUTS = (0, 512, 896)


def pairs(cuts):
    return list(zip(cuts[:-1], cuts[1:]))


def tile_moe_shr_lin_relu_kernel(tc, x_words, x_scales, w, b, gate, offs, pos1, pos2, out):
    nc = tc.nc
    with ExitStack() as ctx:
        keep = ctx.enter_context(tc.tile_pool(name="keep", bufs=1))
        psum = ctx.enter_context(tc.psum_pool(name="psum", bufs=1))

        def ring_bank(name):
            return psum.tile([P, BANK], F32, name=name, tag="ring", bufs=8 - len(pairs(SUM_CUTS)))

        offs_sb = keep.tile([P, S // LANES], U16, name="offs_sb")
        pos_sb = [keep.tile([P, T // LANES], U16, name="pos%d_sb" % r) for r in (1, 2)]
        x_sb = [keep.tile([P, T], I32, name="x_sb%d" % o, align_bytes=64) for o in range(PASSES)]
        xs_sb = keep.tile([P, T], U8, name="xs_sb", align_bytes=64)
        raw = [keep.tile([P, PASSES, PACK, N], F32, name="raw%d" % e, tag="raw%d" % e, align_bytes=64) for e in range(E + 1)]
        b_sb = keep.tile([P, E + 1], F32, name="b_sb")
        gate_rows = keep.tile([P, P], F32, name="gate_rows")
        gate_tail = keep.tile([P, 2, T - TURNED], F32, name="gate_tail")
        ident = keep.tile([P, P], F32, name="ident")

        def load_x(o):
            nc.sync.dma_start(x_sb[o][:], x_words[o].rearrange("p t r -> p (t r)").bitcast(I32))

        def load_w(e):
            nc.sync.dma_start(raw[e][:], w[e].rearrange("(o p j) n -> p o j n", o=PASSES, j=PACK))

        nc.vector.memset(xs_sb[:].bitcast(I32), 0)
        nc.gpsimd.memset(gate_rows[:], 0.0)
        make_identity(nc, ident[:])
        nc.sync.dma_start(offs_sb[:], offs)
        load_x(0)
        for q in range(4):
            nc.scalar.dma_start(
                xs_sb[32 * q : 32 * q + 4 * PASSES, :].bitcast(I32),
                x_scales[:, 4 * q : 4 * q + 4, :].bitcast(I32),
            )
        for e in (E, 0, 1):
            load_w(e)
        nc.sync.dma_start(b_sb[:], b)
        nc.sync.dma_start(gate_rows[0 : 2 * BLOCKS, :], gate[:, 0, 0:TURNED].rearrange("r (c p) -> r c p", p=P))
        load_w(2)
        load_x(1)
        for e in range(3, 6):
            load_w(e)
        load_x(2)
        for e in range(6, E):
            load_w(e)
        nc.sync.dma_start(pos_sb[0][:], pos1)
        nc.sync.dma_start(pos_sb[1][:], pos2)
        nc.sync.dma_start(gate_tail[:], gate[:, :, TURNED:T].rearrange("r p t -> p r t"))

        g_words = [keep.tile([P, S], U32, name="g_words%d" % o, align_bytes=64) for o in range(PASSES - 1)]
        g_words.append(keep.tile([P, S - C], U32, name="g_words_last", align_bytes=64))
        g_scales = keep.tile([P, S], U8, name="g_scales", align_bytes=64)

        def gather(dst, window, cuts, first=0):
            for lo, hi in pairs(cuts):
                nc.vector.tensor_copy(dst[:, lo - first : hi - first], window.indirect(offs_sb[:, lo // LANES : hi // LANES]))

        w_codes = [keep.tile([P, PASSES * N], U32, name="w_codes%d" % e, align_bytes=64) for e in range(E + 1)]
        w_scales = [keep.tile([P, PASSES * N], U8, name="w_scales%d" % e, align_bytes=64) for e in range(E + 1)]
        grouped = [keep.tile([P, K], BF16, name="grouped%d" % e, tag="grouped%d" % e, align_bytes=64) for e in range(E + 1)]

        def cast(e):
            nc.scalar.copy(
                grouped[e][:].rearrange("p (o c i j) -> p o c j i", o=PASSES, i=4, j=PACK),
                raw[e][:].rearrange("p o j (c i) -> p o c j i", i=4),
            )

        def quantize(e):
            for lo, hi in ((0, 1024), (1024, K)):
                nc.vector.quantize_mx(
                    out=w_codes[e][:, lo // PACK : hi // PACK].bitcast(FP8X4),
                    scales=w_scales[e][:, lo // PACK : hi // PACK],
                    in_=grouped[e][:, lo:hi],
                )

        def multiply(acc, e, words, scales, cols):
            for o in range(PASSES):
                nc.tensor.matmul_mx(
                    out=acc,
                    lhsT=w_codes[e][:, o * N : (o + 1) * N].bitcast(FP8X4),
                    lhsT_scale=w_scales[e][:, o * N : (o + 1) * N],
                    rhs=words[o].bitcast(FP8X4),
                    rhs_scale=scales[4 * o : P, cols],
                    start=(o == 0),
                    stop=(o == PASSES - 1),
                )

        for e in [E] + list(range(E)):
            cast(e)
        gather(g_words[0], x_sb[0][:].bitcast(U32), GATHER_CUTS)
        gather(g_scales, xs_sb[:], GATHER_CUTS)
        for e in (E, 0, 1, 2):
            quantize(e)
        gather(g_words[1], x_sb[1][:].bitcast(U32), GATHER_CUTS)
        for e in range(3, 6):
            quantize(e)
        gather(g_words[2], x_sb[2][:].bitcast(U32), LAST_CUTS)
        for e in range(6, E):
            quantize(e)
        g_end = keep.tile([P, C], U32, name="g_end", tag="grouped%d" % (E - 1), align_bytes=64)
        gather(g_end, x_sb[2][:].bitcast(U32), (S - C, S), first=S - C)

        gate_bank = ring_bank("gate_bank")
        nc.tensor.transpose(gate_bank[:, :P], gate_rows[:], ident[:])
        gate_cols = keep.tile([P, 16], F32, name="gate_cols")
        nc.scalar.copy(gate_cols[:], gate_bank[:, :16])

        ys = keep.tile([P, T], F32, name="ys")
        for lo in range(0, T, BANK):
            cols = slice(lo, min(lo + BANK, T))
            width = cols.stop - lo
            acc_s = ring_bank("acc_s")
            multiply(acc_s[:, :width], E, [x_sb[o][:, cols] for o in range(PASSES)], xs_sb, cols)
            nc.scalar.activation(ys[:, cols], acc_s[:, :width], RELU, bias=b_sb[:, E : E + 1])
        ys_t = keep.tile([P, TURNED], F32, name="ys_t")
        for lo in range(0, TURNED, BANK):
            width = min(BANK, TURNED - lo)
            ys_bank = ring_bank("ys_bank")
            for c in range(0, width, P):
                nc.tensor.transpose(ys_bank[:, c : c + P], ys[:, lo + c : lo + c + P], ident[:])
            nc.scalar.copy(ys_t[:, lo : lo + width], ys_bank[:, :width])
        totals = {}
        for lo, hi in pairs(SUM_CUTS):
            totals[lo] = psum.tile([P, BANK], F32, name="total%d" % lo)
            for c in range(lo, hi, P):
                nc.tensor.matmul(
                    totals[lo][:, c - lo : c - lo + P], ys_t[:, c : c + P], ident[:],
                    is_transpose=True, start=(c == lo), stop=False,
                )

        y = keep.tile([P, S], F32, name="y", tag="raw%d" % (E - 1), align_bytes=64)
        for e in range(E - 1):
            acc = ring_bank("acc")
            cols = slice(e * C, (e + 1) * C)
            multiply(acc[:, :C], e, [g_words[o][:, cols] for o in range(PASSES)], g_scales, cols)
            nc.scalar.activation(y[:, cols], acc[:, :C], RELU, bias=b_sb[:, e : e + 1])
        for h in range(2):
            acc = ring_bank("acc")
            cols = slice(S - C + h * P, S - C + (h + 1) * P)
            words = [g_words[0][:, cols], g_words[1][:, cols], g_end[:, h * P : (h + 1) * P]]
            multiply(acc[:, :P], E - 1, words, g_scales, cols)
            if h == 0:
                nc.scalar.activation(y[:, cols], acc[:, :P], RELU, bias=b_sb[:, E - 1 : E])
            else:
                nc.vector.tensor_scalar(y[:, cols], acc[:, :P], b_sb[:, E - 1 : E], 0.0, ADD, MAX)

        fetched = [keep.tile([P, T], F32, name="fetched%d" % r) for r in range(2)]
        scaled = [keep.tile([P, TURNED], F32, name="scaled%d" % r) for r in range(2)]
        res = keep.tile([P, T], F32, name="res")
        for f_lo, f_hi in pairs(FETCH_CUTS):
            for r in range(2):
                nc.vector.tensor_copy(
                    fetched[r][:, f_lo:f_hi], y[:].indirect(pos_sb[r][:, f_lo // LANES : f_hi // LANES])
                )
            chunks = [(lo, hi) for lo, hi in pairs(SUM_CUTS) if f_lo <= lo and hi <= f_hi]
            for r in range(2):
                for lo, hi in chunks:
                    width = P if (r == 1 and hi == TURNED) else hi - lo
                    for start in range(lo, hi, width):
                        turned = ring_bank("turned")
                        for c in range(start, start + width, P):
                            nc.tensor.transpose(turned[:, c - start : c - start + P], fetched[r][:, c : c + P], ident[:])
                        for c in range(start, start + width, P):
                            col = BLOCKS * r + c // P
                            nc.scalar.activation(
                                scaled[r][:, c : c + P], turned[:, c - start : c - start + P], COPY,
                                scale=gate_cols[:, col : col + 1],
                            )
                    for c in range(lo, hi, P):
                        nc.tensor.matmul(
                            totals[lo][:, c - lo : c - lo + P], scaled[r][:, c : c + P], ident[:],
                            is_transpose=True, start=False, stop=(r == 1 and c == hi - P),
                        )
                    if r == 1:
                        nc.scalar.copy(res[:, lo:hi], totals[lo][:, : hi - lo])
                        queue = nc.scalar if hi == TURNED else nc.sync
                        queue.dma_start(out[:, lo:hi], res[:, lo:hi])

        def fetch_gated(r, lo, hi):
            nc.vector.tensor_tensor(
                fetched[r][:, lo:hi], y[:].indirect(pos_sb[r][:, lo // LANES : hi // LANES]),
                gate_tail[:, r, lo - TURNED : hi - TURNED], MULT,
            )

        part = keep.tile([P, T - TURNED], F32, name="part")
        mid = T - P
        fetch_gated(0, TURNED, T)
        fetch_gated(1, TURNED, mid)
        nc.vector.tensor_tensor(part[:], fetched[0][:, TURNED:T], ys[:, TURNED:T], ADD)
        fetch_gated(1, mid, T)
        for lo, hi in ((TURNED, mid), (mid, T)):
            nc.vector.tensor_tensor(res[:, lo:hi], part[:, lo - TURNED : hi - TURNED], fetched[1][:, lo:hi], ADD)
            nc.sync.dma_start(out[:, lo:hi], res[:, lo:hi])
